import numpy as np
import ml_dtypes


def mxq(x, axis, fmt="e4m3"):
    dtype, down = {"e4m3": (ml_dtypes.float8_e4m3fn, 7), "e5m2": (ml_dtypes.float8_e5m2, 14)}[fmt]
    v = np.moveaxis(np.asarray(x, np.float32).astype(ml_dtypes.bfloat16).astype(np.float64), axis, -1)
    blocks = v.reshape(v.shape[:-1] + (-1, 32))
    amax = np.abs(blocks).max(-1, keepdims=True)
    byte = np.maximum(np.where(amax > 0, np.frexp(amax)[1] - 1 + 127, 0) - down, 1)
    scale = np.exp2(byte - 127.0)
    codes = (blocks / scale).astype(np.float32).astype(dtype).astype(np.float64)
    return np.moveaxis((codes * scale).reshape(v.shape), -1, axis)


WIDE = False


def mx_kscale(k):
    if not WIDE:
        return np.ones(k)
    levels = np.array([10, -10, 5, -5, 0])
    if k % 512:
        return np.exp2(np.random.permutation(np.resize(levels, k // 32))).repeat(32)
    a = np.empty((k // 512, 16))
    for p in range(k // 512):
        a[p, :8] = np.random.permutation(np.resize(levels, 8))
        for g in range(8):
            far = levels[np.abs(levels - a[p, g]) >= 10]
            a[p, g + 8] = far[np.random.randint(len(far))]
    return np.exp2(a.ravel()).repeat(32)


def f64(x):
    return np.asarray(x).astype(np.float64)


def striped8(idx):
    return np.asarray(idx).reshape(8, -1, 16).transpose(0, 2, 1).reshape(128, -1).astype(np.uint16)


def unstriped8(offs):
    return offs.reshape(8, 16, -1).transpose(0, 2, 1).reshape(8, -1).astype(np.int64)


def pick8(x, idx, run):
    r = np.arange(len(x))
    return x[r[:, None], idx[r % (8 * run) // run]]


E2M1 = np.array([0.0, 0.5, 1.0, 1.5, 2.0, 3.0, 4.0, 6.0, -0.0, -0.5, -1.0, -1.5, -2.0, -3.0, -4.0, -6.0])


def pack_weight(w, fmt):
    k, n = w.shape
    w = f64(np.asarray(w, np.float32).astype(ml_dtypes.bfloat16)).reshape(k // 32, 32, n)
    amax = np.abs(w).max(1)
    if fmt == "e4m3":
        byte = np.frexp(amax)[1] - 1 + 127 - 7
    else:
        mant, ex = np.frexp(amax / 6.0)
        byte = np.where(mant > 0.5, ex, ex - 1) + 127
    byte = np.clip(np.where(amax > 0, byte, 1), 1, 254)
    scaled = (w * np.exp2(127.0 - byte)[:, None, :]).reshape(k, n).astype(np.float32)
    by_word = np.ascontiguousarray(scaled.reshape(k // 512, 128, 4, n).transpose(0, 1, 3, 2))
    if fmt == "e4m3":
        words = by_word.astype(ml_dtypes.float8_e4m3fn).view(np.uint8)
    else:
        c = by_word.astype(ml_dtypes.float4_e2m1fn).view(np.uint8) & 0xF
        words = (c[..., 0::2] | (c[..., 1::2] << 4)).reshape(k // 512, 128, 2 * n)
    return np.ascontiguousarray(words), np.ascontiguousarray(byte.astype(np.uint8).reshape(k // 512, 16, n))


def unpack_weight(words, scales, fmt):
    g, _, n = scales.shape
    words = np.ascontiguousarray(words).reshape(g, 128, n, -1)
    if fmt == "e4m3":
        vals = words.view(ml_dtypes.float8_e4m3fn).astype(np.float64)
    else:
        nib = np.empty((g, 128, n, 4), np.uint8)
        nib[..., 0::2] = words & 0xF
        nib[..., 1::2] = words >> 4
        vals = E2M1[nib]
    vals = vals * np.repeat(np.exp2(scales.astype(np.float64) - 127.0), 8, axis=1)[..., None]
    return vals.transpose(0, 1, 3, 2).reshape(g * 512, n)


D, T, I, Q = 512, 1024, 512, 128


def setup_inputs():
    n = np.random.standard_normal
    idx = np.stack([np.random.permutation(T)[:I] for _ in range(8)])
    idx2 = np.stack([np.random.permutation(T)[:I] for _ in range(8)])
    idx3 = np.stack([np.random.permutation(T)[:I] for _ in range(8)])
    fd = mx_kscale(D)
    keysp = pack_weight(n((D, T)) / fd[:, None], "e4m3")
    return {
        "query": (n((D, Q)) * 0.9 / np.sqrt(D) * fd[:, None]).astype(np.float32),
        "query2": (n((D, Q)) * 0.9 / np.sqrt(D) * fd[:, None]).astype(np.float32),
        "keys_words": keysp[0],
        "keys_scales": keysp[1],
        "lam": (np.random.uniform(0.5, 1.5, (Q, 1))).astype(np.float32),
        "old": (1.0 * n((Q, T))).astype(np.float32),
        "offs": striped8(idx),
        "offs2": striped8(idx2),
        "offs3": striped8(idx3),
    }


def reference(query, query2, keys_words, keys_scales, lam, old, offs, offs2, offs3):
    idx = unstriped8(offs)
    idx2 = unstriped8(offs2)
    idx3 = unstriped8(offs3)
    keysu = unpack_weight(keys_words, keys_scales, "e4m3")
    queryq = mxq(f64(query), 0, "e4m3")
    a = queryq.T @ keysu
    query2q = mxq(f64(query2), 0, "e4m3")
    b = query2q.T @ keysu
    w = pick8(a, idx, 16) + pick8(a, idx2, 16) * np.tanh(pick8(b, idx, 16)) * f64(lam)
    f1 = np.zeros((Q, T))
    f1[np.arange(Q)[:, None], idx[np.arange(Q) % 128 // 16]] = w
    f2 = f1 + f64(old)
    y = pick8(f2, idx3, 16) * w
    return y

@@ -1,0 +1,139 @@
+from contextlib import ExitStack
+
+import concourse.mybir as mybir
+
+D, T, SLOTS, Q = 512, 1024, 512, 128
+FLOPS = 2 * 2 * D * Q * T
+
+F32 = mybir.dt.float32
+BF16 = mybir.dt.bfloat16
+I32 = mybir.dt.int32
+U32 = mybir.dt.uint32
+U16 = mybir.dt.uint16
+U8 = mybir.dt.uint8
+FP8X4 = mybir.dt.float8_e4m3fn_x4
+MULT = mybir.AluOpType.mult
+ADD = mybir.AluOpType.add
+COPY = mybir.ActivationFunctionType.Copy
+TANH = mybir.ActivationFunctionType.Tanh
+
+P = 128
+PACK = 4
+QUARTERS = 4
+N = T // QUARTERS
+HALF = SLOTS // 2
+LIST_COLS = HALF // 16
+
+
+def tile_attend_turnedby_lean_throughtimes_heads_kernel(
+    tc, query, query2, keys_words, keys_scales, lam, old, offs, offs2, offs3, out
+):
+    nc = tc.nc
+    with ExitStack() as ctx:
+        pool = ctx.enter_context(tc.tile_pool(name="keep", bufs=1))
+        psum = ctx.enter_context(tc.psum_pool(name="psum", bufs=1))
+
+        idx = pool.tile([P, SLOTS // 16], U16, name="idx")
+        idx2 = pool.tile([P, SLOTS // 16], U16, name="idx2")
+        idx3 = pool.tile([P, SLOTS // 16], U16, name="idx3")
+
+        key_scales = pool.tile([P, N], U8, name="key_scales", align_bytes=64)
+        nc.vector.memset(key_scales[:].bitcast(I32), 0)
+        f1 = pool.tile([P, T], F32, name="f1")
+        nc.vector.memset(f1[:], 0.0)
+
+        raw2 = pool.tile([P, PACK, Q], F32, name="raw2")
+        raw1 = pool.tile([P, PACK, Q], F32, name="raw1")
+        words = keys_words[0].rearrange("p n t -> p (n t)").bitcast(I32)
+        key_first = pool.tile([P, 3 * N], U32, name="key_first", align_bytes=64)
+        key_last = pool.tile([P, N], U32, name="key_last", align_bytes=64)
+        key_codes = [key_first[:, j * N : (j + 1) * N] for j in range(3)] + [key_last[:]]
+
+        nc.sync.dma_start(out=raw2[:], in_=query2.rearrange("(p j) q -> p j q", j=PACK))
+        scale_words = keys_scales[0].bitcast(I32)
+        for quad in range(4):
+            nc.sync.dma_start(
+                out=key_scales[32 * quad : 32 * quad + 16, :].bitcast(I32),
+                in_=scale_words[4 * quad : 4 * quad + 4, :].rearrange("r (j c) -> j r c", j=QUARTERS),
+            )
+        nc.sync.dma_start(out=key_first[:].bitcast(I32), in_=words[:, : 3 * N])
+        nc.sync.dma_start(out=raw1[:], in_=query.rearrange("(p j) q -> p j q", j=PACK))
+        nc.sync.dma_start(out=key_last[:].bitcast(I32), in_=words[:, 3 * N :])
+        nc.sync.dma_start(idx[:], offs)
+        nc.sync.dma_start(idx2[:], offs2)
+        lam_col = pool.tile([P, 1], F32, name="lam_col")
+        nc.sync.dma_start(out=lam_col[:], in_=lam)
+        nc.sync.dma_start(idx3[:], offs3)
+        old_sb = pool.tile([P, T], F32, name="old_sb")
+        nc.sync.dma_start(out=old_sb[:], in_=old)
+
+        def quantise(raw, name):
+            grouped = pool.tile([P, Q, PACK], BF16, name=name + "_bf16", align_bytes=64)
+            codes = pool.tile([P, Q], U32, name=name + "_codes", align_bytes=64)
+            scales = pool.tile([P, Q], U8, name=name + "_scales", align_bytes=64)
+            parts = [slice(0, Q // 2), slice(Q // 2, Q)]
+            for cols in parts:
+                nc.vector.tensor_copy(out=grouped[:, cols, :], in_=raw[:, :, cols].rearrange("p j q -> p q j"))
+            for cols in parts:
+                nc.vector.quantize_mx(
+                    out=codes[:, cols].bitcast(FP8X4),
+                    scales=scales[:, cols],
+                    in_=grouped[:, cols, :].rearrange("p q j -> p (q j)"),
+                )
+            return codes, scales
+
+        def score(codes, scales, name, empty_bank):
+            scores = pool.tile([P, T], F32, name=name)
+            for j in range(QUARTERS):
+                bank = psum.tile([P, N], F32, name=f"{name}_bank{j}")
+                nc.tensor.matmul_mx(
+                    out=bank[:],
+                    lhsT=codes[:].bitcast(FP8X4),
+                    lhsT_scale=scales[:],
+                    rhs=key_codes[j].bitcast(FP8X4),
+                    rhs_scale=key_scales[4 * j : P, :],
+                    start=True,
+                    stop=True,
+                )
+                empty_bank(scores[:, j * N : (j + 1) * N], bank[:])
+            return scores
+
+        codes2, scales2 = quantise(raw2, "q2")
+        codes1, scales1 = quantise(raw1, "q1")
+        b = score(codes2, scales2, "b", lambda dst, src: nc.scalar.activation(dst, src, COPY))
+        a = score(codes1, scales1, "a", nc.vector.tensor_copy)
+
+        def half(lists, h):
+            return lists[:, h * LIST_COLS : (h + 1) * LIST_COLS]
+
+        def slots(name):
+            return pool.tile([P, HALF], F32, name=name)
+
+        b0, b1, t0, t1, s0, s1, g0, g1, w0, w1 = (
+            slots(n)[:] for n in ("b0", "b1", "t0", "t1", "s0", "s1", "g0", "g1", "w0", "w1")
+        )
+        a0, a1 = b0, b1
+        nc.scalar.activation(b0, b[:].indirect(half(idx, 0)), COPY)
+        nc.scalar.activation(b1, b[:].indirect(half(idx, 1)), COPY)
+        nc.scalar.activation(t0, b0, TANH)
+        nc.scalar.activation(t1, b1, TANH)
+        nc.scalar.activation(a0, a[:].indirect(half(idx, 0)), COPY)
+        nc.scalar.activation(a1, a[:].indirect(half(idx, 1)), COPY)
+        nc.vector.tensor_copy(s0, a[:].indirect(half(idx2, 0)))
+        nc.vector.tensor_copy(s1, a[:].indirect(half(idx2, 1)))
+        nc.vector.scalar_tensor_tensor(g0, t0, lam_col[:], s0, MULT, MULT)
+        nc.vector.scalar_tensor_tensor(g1, t1, lam_col[:], s1, MULT, MULT)
+        nc.vector.tensor_tensor(f1[:].indirect(half(idx, 0)), g0, a0, ADD)
+        nc.vector.tensor_tensor(w0, g0, a0, ADD)
+        nc.vector.tensor_tensor(f1[:].indirect(half(idx, 1)), g1, a1, ADD)
+        nc.vector.tensor_tensor(w1, g1, a1, ADD)
+
+        f2 = pool.tile([P, T], F32, name="f2")
+        nc.vector.tensor_tensor(f2[:], f1[:], old_sb[:], ADD)
+
+        y0, y1, f21 = (slots(n) for n in ("y0", "y1", "f21"))
+        nc.vector.tensor_tensor(y0[:], f2[:].indirect(half(idx3, 0)), w0, MULT)
+        nc.scalar.activation(f21[:], f2[:].indirect(half(idx3, 1)), COPY)
+        nc.sync.dma_start(out=out[:, :HALF], in_=y0[:])
+        nc.vector.tensor_tensor(y1[:], f21[:], w1, MULT)
+        nc.sync.dma_start(out=out[:, HALF:], in_=y1[:])

@@ -1,6 +1,7 @@
 from contextlib import ExitStack
 
 import concourse.mybir as mybir
+from concourse.masks import make_identity
 
 D, T, SLOTS, Q = 512, 1024, 512, 128
 FLOPS = 2 * 2 * D * Q * T
@@ -23,6 +24,8 @@ QUARTERS = 4
 N = T // QUARTERS
 HALF = SLOTS // 2
 LIST_COLS = HALF // 16
+BANK = 512
+VECTOR_COLS = 640
 
 
 def tile_attend_turnedby_lean_throughtimes_heads_kernel(
@@ -68,7 +71,7 @@ def tile_attend_turnedby_lean_throughtimes_heads_kernel(
         nc.sync.dma_start(out=old_sb[:], in_=old)
 
         def quantise(raw, name):
-            grouped = pool.tile([P, Q, PACK], BF16, name=name + "_bf16", align_bytes=64)
+            grouped = pool.tile([P, Q, PACK], BF16, name=name + "_bf16", tag=name + "_bf16", align_bytes=64)
             codes = pool.tile([P, Q], U32, name=name + "_codes", align_bytes=64)
             scales = pool.tile([P, Q], U8, name=name + "_scales", align_bytes=64)
             parts = [slice(0, Q // 2), slice(Q // 2, Q)]
@@ -85,7 +88,7 @@ def tile_attend_turnedby_lean_throughtimes_heads_kernel(
         def score(codes, scales, name, empty_bank):
             scores = pool.tile([P, T], F32, name=name)
             for j in range(QUARTERS):
-                bank = psum.tile([P, N], F32, name=f"{name}_bank{j}")
+                bank = psum.tile([P, N], F32, name=f"{name}_bank{j}", tag=f"{name}{j}")
                 nc.tensor.matmul_mx(
                     out=bank[:],
                     lhsT=codes[:].bitcast(FP8X4),
@@ -109,9 +112,11 @@ def tile_attend_turnedby_lean_throughtimes_heads_kernel(
         def slots(name):
             return pool.tile([P, HALF], F32, name=name)
 
-        b0, b1, t0, t1, s0, s1, g0, g1, w0, w1 = (
-            slots(n)[:] for n in ("b0", "b1", "t0", "t1", "s0", "s1", "g0", "g1", "w0", "w1")
+        b0, b1, s0, s1, g0, g1, w0, w1 = (
+            slots(n)[:] for n in ("b0", "b1", "s0", "s1", "g0", "g1", "w0", "w1")
         )
+        t = pool.tile([P, SLOTS], F32, name="t")
+        t0, t1 = t[:, :HALF], t[:, HALF:]
         a0, a1 = b0, b1
         nc.scalar.activation(b0, b[:].indirect(half(idx, 0)), COPY)
         nc.scalar.activation(b1, b[:].indirect(half(idx, 1)), COPY)
@@ -129,7 +134,19 @@ def tile_attend_turnedby_lean_throughtimes_heads_kernel(
         nc.vector.tensor_tensor(w1, g1, a1, ADD)
 
         f2 = pool.tile([P, T], F32, name="f2")
-        nc.vector.tensor_tensor(f2[:], f1[:], old_sb[:], ADD)
+        identity = pool.tile([P, P], F32, name="identity", tag="q1_bf16", align_bytes=64)
+        make_identity(nc, identity[:])
+        stretches = [(0, BANK, t[:]), (BANK, VECTOR_COLS, s1[:, : VECTOR_COLS - BANK])]
+        for n, (first, last, turned) in enumerate(stretches):
+            there = psum.tile([P, last - first], F32, name=f"there{n}", tag=f"a{n}")
+            back = psum.tile([P, last - first], F32, name=f"back{n}", tag=f"b{n}")
+            for c in range(0, last - first, P):
+                nc.tensor.transpose(there[:, c : c + P], old_sb[:, first + c : first + c + P], identity[:])
+            nc.scalar.activation(turned, there[:], COPY)
+            for c in range(0, last - first, P):
+                nc.tensor.transpose(back[:, c : c + P], turned[:, c : c + P], identity[:])
+            nc.vector.tensor_tensor(f2[:, first:last], f1[:, first:last], back[:], ADD)
+        nc.gpsimd.tensor_tensor(f2[:, VECTOR_COLS:], f1[:, VECTOR_COLS:], old_sb[:, VECTOR_COLS:], ADD)
 
         y0, y1, f21 = (slots(n) for n in ("y0", "y1", "f21"))
         nc.vector.tensor_tensor(y0[:], f2[:].indirect(half(idx3, 0)), w0, MULT)

@@ -25,7 +25,7 @@ N = T // QUARTERS
 HALF = SLOTS // 2
 LIST_COLS = HALF // 16
 BANK = 512
-VECTOR_COLS = 640
+VECTOR_COLS = 768
 
 
 def tile_attend_turnedby_lean_throughtimes_heads_kernel(
@@ -41,7 +41,9 @@ def tile_attend_turnedby_lean_throughtimes_heads_kernel(
         idx3 = pool.tile([P, SLOTS // 16], U16, name="idx3")
 
         key_scales = pool.tile([P, N], U8, name="key_scales", align_bytes=64)
-        nc.vector.memset(key_scales[:].bitcast(I32), 0)
+        nc.gpsimd.memset(key_scales[:].bitcast(I32), 0)
+        identity = pool.tile([P, P], F32, name="identity")
+        make_identity(nc, identity[:])
         f1 = pool.tile([P, T], F32, name="f1")
         nc.vector.memset(f1[:], 0.0)
 
@@ -85,26 +87,31 @@ def tile_attend_turnedby_lean_throughtimes_heads_kernel(
                 )
             return codes, scales
 
-        def score(codes, scales, name, empty_bank):
+        def score(codes, scales, name, passes, empty_bank):
             scores = pool.tile([P, T], F32, name=name)
-            for j in range(QUARTERS):
-                bank = psum.tile([P, N], F32, name=f"{name}_bank{j}", tag=f"{name}{j}")
+            for first, last, tag in passes:
+                j = first // N
+                cols = slice(first - j * N, last - j * N)
+                bank = psum.tile([P, last - first], F32, name=f"{name}_bank{first}", tag=tag)
                 nc.tensor.matmul_mx(
                     out=bank[:],
                     lhsT=codes[:].bitcast(FP8X4),
                     lhsT_scale=scales[:],
-                    rhs=key_codes[j].bitcast(FP8X4),
-                    rhs_scale=key_scales[4 * j : P, :],
+                    rhs=key_codes[j][:, cols].bitcast(FP8X4),
+                    rhs_scale=key_scales[4 * j : P, cols],
                     start=True,
                     stop=True,
                 )
-                empty_bank(scores[:, j * N : (j + 1) * N], bank[:])
+                empty_bank(scores[:, first:last], bank[:])
             return scores
 
         codes2, scales2 = quantise(raw2, "q2")
         codes1, scales1 = quantise(raw1, "q1")
-        b = score(codes2, scales2, "b", lambda dst, src: nc.scalar.activation(dst, src, COPY))
-        a = score(codes1, scales1, "a", nc.vector.tensor_copy)
+        b_passes = [(j * N, (j + 1) * N, f"b{j}") for j in range(QUARTERS)]
+        a_passes = [(j * N, (j + 1) * N, f"a{j}") for j in range(QUARTERS - 1)]
+        a_passes += [(T - N, T - N // 2, "a3"), (T - N // 2, T, "b0")]
+        b = score(codes2, scales2, "b", b_passes, lambda dst, src: nc.scalar.activation(dst, src, COPY))
+        a = score(codes1, scales1, "a", a_passes, nc.vector.tensor_copy)
 
         def half(lists, h):
             return lists[:, h * LIST_COLS : (h + 1) * LIST_COLS]
@@ -134,12 +141,10 @@ def tile_attend_turnedby_lean_throughtimes_heads_kernel(
         nc.vector.tensor_tensor(w1, g1, a1, ADD)
 
         f2 = pool.tile([P, T], F32, name="f2")
-        identity = pool.tile([P, P], F32, name="identity", tag="q1_bf16", align_bytes=64)
-        make_identity(nc, identity[:])
         stretches = [(0, BANK, t[:]), (BANK, VECTOR_COLS, s1[:, : VECTOR_COLS - BANK])]
         for n, (first, last, turned) in enumerate(stretches):
             there = psum.tile([P, last - first], F32, name=f"there{n}", tag=f"a{n}")
-            back = psum.tile([P, last - first], F32, name=f"back{n}", tag=f"b{n}")
+            back = psum.tile([P, last - first], F32, name=f"back{n}", tag=f"b{n + 1}")
             for c in range(0, last - first, P):
                 nc.tensor.transpose(there[:, c : c + P], old_sb[:, first + c : first + c + P], identity[:])
             nc.scalar.activation(turned, there[:], COPY)
@@ -149,8 +154,11 @@ def tile_attend_turnedby_lean_throughtimes_heads_kernel(
         nc.gpsimd.tensor_tensor(f2[:, VECTOR_COLS:], f1[:, VECTOR_COLS:], old_sb[:, VECTOR_COLS:], ADD)
 
         y0, y1, f21 = (slots(n) for n in ("y0", "y1", "f21"))
-        nc.vector.tensor_tensor(y0[:], f2[:].indirect(half(idx3, 0)), w0, MULT)
         nc.scalar.activation(f21[:], f2[:].indirect(half(idx3, 1)), COPY)
-        nc.sync.dma_start(out=out[:, :HALF], in_=y0[:])
+        for first in range(0, HALF, HALF // 2):
+            cols = slice(first, first + HALF // 2)
+            listed = idx3[:, first // 16 : (first + HALF // 2) // 16]
+            nc.vector.tensor_tensor(y0[:, cols], f2[:].indirect(listed), w0[:, cols], MULT)
+            nc.sync.dma_start(out=out[:, cols], in_=y0[:, cols])
         nc.vector.tensor_tensor(y1[:], f21[:], w1, MULT)
         nc.sync.dma_start(out=out[:, HALF:], in_=y1[:])

from contextlib import ExitStack

import concourse.mybir as mybir
from concourse.masks import make_identity

D, T, SLOTS, Q = 512, 1024, 512, 128
FLOPS = 2 * 2 * D * Q * T

F32 = mybir.dt.float32
BF16 = mybir.dt.bfloat16
I32 = mybir.dt.int32
U32 = mybir.dt.uint32
U16 = mybir.dt.uint16
U8 = mybir.dt.uint8
FP8X4 = mybir.dt.float8_e4m3fn_x4
MULT = mybir.AluOpType.mult
ADD = mybir.AluOpType.add
COPY = mybir.ActivationFunctionType.Copy
TANH = mybir.ActivationFunctionType.Tanh

P = 128
PACK = 4
QUARTERS = 4
N = T // QUARTERS
HALF = SLOTS // 2
LIST_COLS = HALF // 16
BANK = 512
VECTOR_COLS = 768


def tile_attend_turnedby_lean_throughtimes_heads_kernel(
    tc, query, query2, keys_words, keys_scales, lam, old, offs, offs2, offs3, out
):
    nc = tc.nc
    with ExitStack() as ctx:
        pool = ctx.enter_context(tc.tile_pool(name="keep", bufs=1))
        psum = ctx.enter_context(tc.psum_pool(name="psum", bufs=1))

        idx = pool.tile([P, SLOTS // 16], U16, name="idx")
        idx2 = pool.tile([P, SLOTS // 16], U16, name="idx2")
        idx3 = pool.tile([P, SLOTS // 16], U16, name="idx3")

        key_scales = pool.tile([P, N], U8, name="key_scales", align_bytes=64)
        nc.gpsimd.memset(key_scales[:].bitcast(I32), 0)
        identity = pool.tile([P, P], F32, name="identity")
        make_identity(nc, identity[:])
        f1 = pool.tile([P, T], F32, name="f1")
        nc.vector.memset(f1[:], 0.0)

        raw2 = pool.tile([P, PACK, Q], F32, name="raw2")
        raw1 = pool.tile([P, PACK, Q], F32, name="raw1")
        words = keys_words[0].rearrange("p n t -> p (n t)").bitcast(I32)
        key_first = pool.tile([P, 3 * N], U32, name="key_first", align_bytes=64)
        key_last = pool.tile([P, N], U32, name="key_last", align_bytes=64)
        key_codes = [key_first[:, j * N : (j + 1) * N] for j in range(3)] + [key_last[:]]

        nc.sync.dma_start(out=raw2[:], in_=query2.rearrange("(p j) q -> p j q", j=PACK))
        scale_words = keys_scales[0].bitcast(I32)
        for quad in range(4):
            nc.sync.dma_start(
                out=key_scales[32 * quad : 32 * quad + 16, :].bitcast(I32),
                in_=scale_words[4 * quad : 4 * quad + 4, :].rearrange("r (j c) -> j r c", j=QUARTERS),
            )
        nc.sync.dma_start(out=key_first[:].bitcast(I32), in_=words[:, : 3 * N])
        nc.sync.dma_start(out=raw1[:], in_=query.rearrange("(p j) q -> p j q", j=PACK))
        nc.sync.dma_start(out=key_last[:].bitcast(I32), in_=words[:, 3 * N :])
        nc.sync.dma_start(idx[:], offs)
        nc.sync.dma_start(idx2[:], offs2)
        lam_col = pool.tile([P, 1], F32, name="lam_col")
        nc.sync.dma_start(out=lam_col[:], in_=lam)
        nc.sync.dma_start(idx3[:], offs3)
        old_sb = pool.tile([P, T], F32, name="old_sb")
        nc.sync.dma_start(out=old_sb[:], in_=old)

        def quantise(raw, name):
            grouped = pool.tile([P, Q, PACK], BF16, name=name + "_bf16", tag=name + "_bf16", align_bytes=64)
            codes = pool.tile([P, Q], U32, name=name + "_codes", align_bytes=64)
            scales = pool.tile([P, Q], U8, name=name + "_scales", align_bytes=64)
            parts = [slice(0, Q // 2), slice(Q // 2, Q)]
            for cols in parts:
                nc.vector.tensor_copy(out=grouped[:, cols, :], in_=raw[:, :, cols].rearrange("p j q -> p q j"))
            for cols in parts:
                nc.vector.quantize_mx(
                    out=codes[:, cols].bitcast(FP8X4),
                    scales=scales[:, cols],
                    in_=grouped[:, cols, :].rearrange("p q j -> p (q j)"),
                )
            return codes, scales

        def score(codes, scales, name, passes, empty_bank):
            scores = pool.tile([P, T], F32, name=name)
            for first, last, tag in passes:
                j = first // N
                cols = slice(first - j * N, last - j * N)
                bank = psum.tile([P, last - first], F32, name=f"{name}_bank{first}", tag=tag)
                nc.tensor.matmul_mx(
                    out=bank[:],
                    lhsT=codes[:].bitcast(FP8X4),
                    lhsT_scale=scales[:],
                    rhs=key_codes[j][:, cols].bitcast(FP8X4),
                    rhs_scale=key_scales[4 * j : P, cols],
                    start=True,
                    stop=True,
                )
                empty_bank(scores[:, first:last], bank[:])
            return scores

        codes2, scales2 = quantise(raw2, "q2")
        codes1, scales1 = quantise(raw1, "q1")
        b_passes = [(j * N, (j + 1) * N, f"b{j}") for j in range(QUARTERS)]
        a_passes = [(j * N, (j + 1) * N, f"a{j}") for j in range(QUARTERS - 1)]
        a_passes += [(T - N, T - N // 2, "a3"), (T - N // 2, T, "b0")]
        b = score(codes2, scales2, "b", b_passes, lambda dst, src: nc.scalar.activation(dst, src, COPY))
        a = score(codes1, scales1, "a", a_passes, nc.vector.tensor_copy)

        def half(lists, h):
            return lists[:, h * LIST_COLS : (h + 1) * LIST_COLS]

        def slots(name):
            return pool.tile([P, HALF], F32, name=name)

        b0, b1, s0, s1, g0, g1, w0, w1 = (
            slots(n)[:] for n in ("b0", "b1", "s0", "s1", "g0", "g1", "w0", "w1")
        )
        t = pool.tile([P, SLOTS], F32, name="t")
        t0, t1 = t[:, :HALF], t[:, HALF:]
        a0, a1 = b0, b1
        nc.scalar.activation(b0, b[:].indirect(half(idx, 0)), COPY)
        nc.scalar.activation(b1, b[:].indirect(half(idx, 1)), COPY)
        nc.scalar.activation(t0, b0, TANH)
        nc.scalar.activation(t1, b1, TANH)
        nc.scalar.activation(a0, a[:].indirect(half(idx, 0)), COPY)
        nc.scalar.activation(a1, a[:].indirect(half(idx, 1)), COPY)
        nc.vector.tensor_copy(s0, a[:].indirect(half(idx2, 0)))
        nc.vector.tensor_copy(s1, a[:].indirect(half(idx2, 1)))
        nc.vector.scalar_tensor_tensor(g0, t0, lam_col[:], s0, MULT, MULT)
        nc.vector.scalar_tensor_tensor(g1, t1, lam_col[:], s1, MULT, MULT)
        nc.vector.tensor_tensor(f1[:].indirect(half(idx, 0)), g0, a0, ADD)
        nc.vector.tensor_tensor(w0, g0, a0, ADD)
        nc.vector.tensor_tensor(f1[:].indirect(half(idx, 1)), g1, a1, ADD)
        nc.vector.tensor_tensor(w1, g1, a1, ADD)

        f2 = pool.tile([P, T], F32, name="f2")
        stretches = [(0, BANK, t[:]), (BANK, VECTOR_COLS, s1[:, : VECTOR_COLS - BANK])]
        for n, (first, last, turned) in enumerate(stretches):
            there = psum.tile([P, last - first], F32, name=f"there{n}", tag=f"a{n}")
            back = psum.tile([P, last - first], F32, name=f"back{n}", tag=f"b{n + 1}")
            for c in range(0, last - first, P):
                nc.tensor.transpose(there[:, c : c + P], old_sb[:, first + c : first + c + P], identity[:])
            nc.scalar.activation(turned, there[:], COPY)
            for c in range(0, last - first, P):
                nc.tensor.transpose(back[:, c : c + P], turned[:, c : c + P], identity[:])
            nc.vector.tensor_tensor(f2[:, first:last], f1[:, first:last], back[:], ADD)
        nc.gpsimd.tensor_tensor(f2[:, VECTOR_COLS:], f1[:, VECTOR_COLS:], old_sb[:, VECTOR_COLS:], ADD)

        y0, y1, f21 = (slots(n) for n in ("y0", "y1", "f21"))
        nc.scalar.activation(f21[:], f2[:].indirect(half(idx3, 1)), COPY)
        for first in range(0, HALF, HALF // 2):
            cols = slice(first, first + HALF // 2)
            listed = idx3[:, first // 16 : (first + HALF // 2) // 16]
            nc.vector.tensor_tensor(y0[:, cols], f2[:].indirect(listed), w0[:, cols], MULT)
            nc.sync.dma_start(out=out[:, cols], in_=y0[:, cols])
        nc.vector.tensor_tensor(y1[:], f21[:], w1, MULT)
        nc.sync.dma_start(out=out[:, HALF:], in_=y1[:])
